import numpy as np
import ml_dtypes


def mxq(x, axis, fmt="e4m3"):
    dtype, down = {"e4m3": (ml_dtypes.float8_e4m3fn, 7), "e5m2": (ml_dtypes.float8_e5m2, 14)}[fmt]
    v = np.moveaxis(np.asarray(x, np.float32).astype(ml_dtypes.bfloat16).astype(np.float64), axis, -1)
    blocks = v.reshape(v.shape[:-1] + (-1, 32))
    amax = np.abs(blocks).max(-1, keepdims=True)
    byte = np.maximum(np.where(amax > 0, np.frexp(amax)[1] - 1 + 127, 0) - down, 1)
    scale = np.exp2(byte - 127.0)
    codes = (blocks / scale).astype(np.float32).astype(dtype).astype(np.float64)
    return np.moveaxis((codes * scale).reshape(v.shape), -1, axis)


WIDE = False


def mx_kscale(k):
    if not WIDE:
        return np.ones(k)
    levels = np.array([10, -10, 5, -5, 0])
    if k % 512:
        return np.exp2(np.random.permutation(np.resize(levels, k // 32))).repeat(32)
    a = np.empty((k // 512, 16))
    for p in range(k // 512):
        a[p, :8] = np.random.permutation(np.resize(levels, 8))
        for g in range(8):
            far = levels[np.abs(levels - a[p, g]) >= 10]
            a[p, g + 8] = far[np.random.randint(len(far))]
    return np.exp2(a.ravel()).repeat(32)


BF16 = ml_dtypes.bfloat16


def bf(x):
    return np.asarray(x, np.float32).astype(BF16)


def f64(x):
    return np.asarray(x).astype(np.float64)


E2M1 = np.array([0.0, 0.5, 1.0, 1.5, 2.0, 3.0, 4.0, 6.0, -0.0, -0.5, -1.0, -1.5, -2.0, -3.0, -4.0, -6.0])


def pack_weight(w, fmt):
    k, n = w.shape
    w = f64(bf(w)).reshape(k // 32, 32, n)
    amax = np.abs(w).max(1)
    if fmt == "e4m3":
        byte = np.frexp(amax)[1] - 1 + 127 - 7
    else:
        mant, ex = np.frexp(amax / 6.0)
        byte = np.where(mant > 0.5, ex, ex - 1) + 127
    byte = np.clip(np.where(amax > 0, byte, 1), 1, 254)
    scaled = (w * np.exp2(127.0 - byte)[:, None, :]).reshape(k, n).astype(np.float32)
    by_word = np.ascontiguousarray(scaled.reshape(k // 512, 128, 4, n).transpose(0, 1, 3, 2))
    if fmt == "e4m3":
        words = by_word.astype(ml_dtypes.float8_e4m3fn).view(np.uint8)
    else:
        c = by_word.astype(ml_dtypes.float4_e2m1fn).view(np.uint8) & 0xF
        words = c[..., 0::2] | (c[..., 1::2] << 4)
    return np.ascontiguousarray(words), np.ascontiguousarray(byte.astype(np.uint8).reshape(k // 512, 16, n))


def unpack_weight(words, scales, fmt):
    g, p, n, _ = words.shape
    if fmt == "e4m3":
        vals = np.ascontiguousarray(words).view(ml_dtypes.float8_e4m3fn).astype(np.float64)
    else:
        nib = np.empty((g, p, n, 4), np.uint8)
        nib[..., 0::2] = words & 0xF
        nib[..., 1::2] = words >> 4
        vals = E2M1[nib]
    vals = vals * np.repeat(np.exp2(scales.astype(np.float64) - 127.0), 8, axis=1)[..., None]
    return vals.transpose(0, 1, 3, 2).reshape(g * 512, n)
def pack4(w):
    words, scales = pack_weight(w, "e2m1")
    return words.reshape(words.shape[0], 128, -1), scales


def unpack4(words, scales):
    return unpack_weight(words.reshape(words.shape[0], 128, -1, 2), scales, "e2m1")


M, A, B, C, T = 1024, 512, 1024, 2048, 512


def setup_inputs():
    sa, sb, u = mx_kscale(A), mx_kscale(B), mx_kscale(C)
    gone_near = np.random.standard_normal((M, A)) * (np.random.uniform(size=(M, A)) < 0.5)
    gone_far = np.random.standard_normal((M, B)) * (np.random.uniform(size=(M, B)) < 0.5)
    far = np.random.standard_normal((B, C)) / np.sqrt(B)
    far_words, far_scales = pack4(far / sb[:, None] * u)
    x_words, x_scales = pack4(np.random.standard_normal((C, T)) / np.sqrt(C) / u[:, None])
    return {"w_rest": bf(np.random.standard_normal((M, C)) * u),
            "gone_near": bf(gone_near * sa),
            "rd_near": bf(np.random.uniform(0.5, 1.5, A)),
            "inv_near": bf(np.random.standard_normal((A, C)) / np.sqrt(A) / sa[:, None] * u),
            "gone_far": bf(gone_far * sb),
            "rd_far": bf(np.random.uniform(0.5, 1.5, B)),
            "far_words": far_words, "far_scales": far_scales,
            "x_words": x_words, "x_scales": x_scales}


def reference(w_rest, gone_near, rd_near, inv_near, gone_far, rd_far, far_words, far_scales, x_words, x_scales):
    e_near = mxq(f64(gone_near) * f64(rd_near), 1, "e4m3")
    e_far = mxq(f64(gone_far) * f64(rd_far), 1, "e4m3")
    delta = (e_near @ mxq(f64(inv_near), 0, "e4m3")) + (e_far @ unpack4(far_words, far_scales))
    updated = f64(w_rest) - delta
    return mxq(updated, 1, "e4m3") @ unpack4(x_words, x_scales)

@@ -1,0 +1,363 @@
+from contextlib import ExitStack
+
+import concourse.mybir as mybir
+from concourse.masks import make_identity
+
+M, A, B, C, T = 1024, 512, 1024, 2048, 512
+FLOPS = 2 * M * (A + B) * C + 2 * M * C * T
+
+F32 = mybir.dt.float32
+BF16 = mybir.dt.bfloat16
+I32 = mybir.dt.int32
+U32 = mybir.dt.uint32
+U8 = mybir.dt.uint8
+FP8X4 = mybir.dt.float8_e4m3fn_x4
+FP4X4 = mybir.dt.float4_e2m1fn_x4
+ALU = mybir.AluOpType
+
+P = 128
+KP = 512
+ROW_TILES = M // P
+CHUNKS = C // KP
+HEAD = 3
+QUAD = 4
+LAG = 3
+SORT_FROM = 4
+VEC_COLS0 = 288
+
+
+def tile_sparsegpt_lazy_update_s3_kernel(
+    tc, w_rest, gone_near, rd_near, inv_near, gone_far, rd_far, far_words, far_scales, x_words, x_scales, out
+):
+    nc = tc.nc
+    units = [(m, c) for c in range(CHUNKS) for m in range(HEAD)]
+    units = units + [(m, c) for m in range(HEAD, ROW_TILES) for c in range(CHUNKS)]
+    quads = [units[i : i + QUAD] for i in range(0, len(units), QUAD)]
+
+    with ExitStack() as ctx:
+        keep = ctx.enter_context(tc.tile_pool(name="keep", bufs=1))
+        stage = ctx.enter_context(tc.tile_pool(name="stage", bufs=2))
+        psum = ctx.enter_context(tc.psum_pool(name="psum", bufs=1))
+        ctx.enter_context(tc.manual_schedule())
+
+        def kept(name, shape, dtype):
+            return keep.tile(shape, dtype, name=name, align_bytes=64)
+
+        def staged(tag, shape, dtype, bufs):
+            return stage.tile(shape, dtype, name=tag, tag=tag, bufs=bufs, align_bytes=64)
+
+        bank_uses = {"acc": 0, "turn": 0}
+
+        def bank(kind, shape):
+            tag = "%s%d" % (kind, bank_uses[kind] % 4)
+            bank_uses[kind] = bank_uses[kind] + 1
+            return psum.tile(shape, F32, name=tag, tag=tag)
+
+        ident = kept("ident", [P, P], F32)
+        make_identity(nc, ident[:])
+
+        far_plane = [kept("far_plane%d" % h, [P, 2, 2 * KP], U8) for h in range(2)]
+        x_plane = kept("x_plane", [P, CHUNKS, T], U8)
+        for h in range(2):
+            nc.vector.memset(far_plane[h][:].bitcast(I32), 0)
+        nc.gpsimd.memset(x_plane[:].bitcast(I32), 0)
+
+        gone = {}
+        rd = {}
+        w_sb = {}
+        inv_raw = {}
+        far_sb = {}
+        passes = {"near": 1, "far": 2}
+        gone_hbm = {"near": gone_near, "far": gone_far}
+
+        def load_rd(part, vec):
+            rd[part] = kept("rd_" + part, [P, passes[part], 1, 4], BF16)
+            nc.scalar.dma_start(out=rd[part][:, :, 0, :], in_=vec.rearrange("(g p t) -> p g t", p=P, t=4))
+
+        def load_gone(m):
+            for part in ("near", "far"):
+                gone[m, part] = kept("gone_%s%d" % (part, m), [P, passes[part] * KP], BF16)
+                nc.sync.dma_start(out=gone[m, part][:], in_=gone_hbm[part][m * P : (m + 1) * P, :])
+
+        def load_inv(c):
+            inv_raw[c] = kept("inv_raw%d" % c, [P, 4, KP], BF16)
+            nc.sync.dma_start(
+                out=inv_raw[c][:], in_=inv_near[:, c * KP : (c + 1) * KP].rearrange("(p t) n -> p t n", t=4)
+            )
+
+        def load_far(c):
+            far_sb[c] = kept("far_sb%d" % c, [P, 2, 2 * KP], U8)
+            nc.sync.dma_start(
+                out=far_sb[c][:].bitcast(I32),
+                in_=far_words.bitcast(I32)[:, :, c * 256 : (c + 1) * 256].rearrange("g p n -> p g n"),
+            )
+
+        def load_scale_rows(queue, plane, rows):
+            for q in range(4):
+                queue.dma_start(
+                    out=plane[32 * q : 32 * q + 4, :, :].bitcast(I32),
+                    in_=rows[:, 4 * q : 4 * q + 4, :].rearrange("g r n -> r g n"),
+                )
+
+        def load_w_head(c):
+            t = kept("w_head%d" % c, [P, HEAD, KP], BF16)
+            nc.sync.dma_start(
+                out=t[:], in_=w_rest[0 : HEAD * P, c * KP : (c + 1) * KP].rearrange("(m p) n -> p m n", p=P)
+            )
+            for m in range(HEAD):
+                w_sb[m, c] = t[:, m, :]
+
+        def load_w(m):
+            t = kept("w_row%d" % m, [P, C], BF16)
+            nc.sync.dma_start(out=t[:], in_=w_rest[m * P : (m + 1) * P, :])
+            for c in range(CHUNKS):
+                w_sb[m, c] = t[:, c * KP : (c + 1) * KP]
+
+        far_rows = far_scales.bitcast(I32)
+        load_rd("near", rd_near)
+        load_rd("far", rd_far)
+        load_gone(0)
+        load_inv(0)
+        load_far(0)
+        load_scale_rows(nc.scalar, far_plane[0], far_rows[:, :, 0:256])
+        load_gone(1)
+        load_inv(1)
+        load_w_head(0)
+        load_gone(2)
+        load_far(1)
+        load_inv(2)
+        load_w_head(1)
+        load_scale_rows(nc.sync, far_plane[1], far_rows[:, :, 256:512])
+        load_far(2)
+        load_inv(3)
+        load_w_head(2)
+        load_far(3)
+        load_gone(3)
+        load_w_head(3)
+        load_w(3)
+        load_gone(4)
+        load_scale_rows(nc.sync, x_plane, x_scales.bitcast(I32))
+        x_sb = kept("x_sb", [P, CHUNKS, 2 * T], U8)
+        nc.sync.dma_start(out=x_sb[:].bitcast(I32), in_=x_words.bitcast(I32).rearrange("g p n -> p g n"))
+        for m in range(4, ROW_TILES):
+            load_w(m)
+            if m + 1 < ROW_TILES:
+                load_gone(m + 1)
+
+        sorted_words = {}
+        e_bank = {}
+        e_bf = {}
+        e_codes = {}
+        inv_bf = {}
+        inv_codes = {}
+        d_bank = {}
+        u_rows = {}
+        u_bank = {}
+        u_bf = {}
+        u_codes = {}
+        y_bank = {}
+
+        def quantize(name, src, width):
+            codes = kept(name + "_codes", [P, width], U32)
+            scales = kept(name + "_scales", [P, width], U8)
+            nc.vector.quantize_mx(out=codes[:].bitcast(FP8X4), scales=scales[:], in_=src)
+            return codes, scales
+
+        def sort_gone(m):
+            for part in ("near", "far"):
+                t = staged("sorted_" + part, [P, passes[part], 2, P], F32, 2)
+                nc.scalar.copy(
+                    out=t[:], in_=gone[m, part][:].bitcast(F32).rearrange("p (g w u) -> p g u w", w=P, u=2)
+                )
+                sorted_words[m, part] = t
+
+        def turn_gone(m):
+            for part in ("near", "far"):
+                b = bank("turn", [P, 2, passes[part], P])
+                for g in range(passes[part]):
+                    for u in range(2):
+                        if m >= SORT_FROM:
+                            src = sorted_words[m, part][:, g, u, :]
+                        else:
+                            src = gone[m, part][:].bitcast(F32)[:, 256 * g + u : 256 * (g + 1) : 2]
+                        nc.tensor.transpose(b[:, u, g, :], src, ident[:])
+                e_bank[m, part] = b
+
+        def scale_errors(m):
+            for part in ("near", "far"):
+                n = passes[part]
+                t = staged("e_bf_" + part, [P, n, P, 4], BF16, 2)
+                nc.vector.tensor_tensor(
+                    out=t[:].rearrange("p g r (u e) -> p (g r) u e", e=2),
+                    in0=e_bank[m, part][:].bitcast(BF16).rearrange("p u g (r e) -> p (g r) u e", e=2),
+                    in1=rd[part][:].broadcast_to([P, n, P, 4]),
+                    op=ALU.mult,
+                )
+                e_bf[m, part] = t
+
+        def quantize_errors(m, part):
+            src = e_bf[m, part][:].rearrange("p g r t -> p (g r t)")
+            e_codes[m, part] = quantize("e_%s%d" % (part, m), src, passes[part] * P)
+
+        def interleave_inv(c, vec_cols):
+            t = staged("inv_bf", [P, KP, 4], BF16, 2)
+            inv_bf[c] = t
+            dst = t[:, vec_cols:KP, :].rearrange("p (n i) t -> p n t i", i=4)
+            nc.scalar.copy(out=dst, in_=inv_raw[c][:, :, vec_cols:KP].rearrange("p t (n i) -> p n t i", i=4))
+            if vec_cols > 0:
+                dst = t[:, 0:vec_cols, :].rearrange("p (n i) t -> p n t i", i=4)
+                nc.vector.tensor_copy(
+                    out=dst, in_=inv_raw[c][:, :, 0:vec_cols].rearrange("p t (n i) -> p n t i", i=4)
+                )
+
+        def quantize_inv(c):
+            inv_codes[c] = quantize("inv%d" % c, inv_bf[c][:].rearrange("p n t -> p (n t)"), KP)
+
+        def far_passes(m, c):
+            d_bank[m, c] = bank("acc", [P, KP])
+            codes, scales = e_codes[m, "far"]
+            for g in range(2):
+                nc.tensor.matmul_mx(
+                    out=d_bank[m, c][:],
+                    lhsT=codes[:, g * P : (g + 1) * P].bitcast(FP8X4),
+                    lhsT_scale=scales[:, g * P : (g + 1) * P],
+                    rhs=far_sb[c][:, g, :].bitcast(FP4X4),
+                    rhs_scale=far_plane[c // 2][:, g, (c % 2) * KP : (c % 2 + 1) * KP],
+                    start=(g == 0),
+                    stop=False,
+                )
+
+        def near_pass(m, c):
+            codes, scales = e_codes[m, "near"]
+            nc.tensor.matmul_mx(
+                out=d_bank[m, c][:],
+                lhsT=codes[:].bitcast(FP8X4),
+                lhsT_scale=scales[:],
+                rhs=inv_codes[c][0][:].bitcast(FP8X4),
+                rhs_scale=inv_codes[c][1][:],
+                start=False,
+                stop=True,
+            )
+
+        def update(unit):
+            far_passes(*unit)
+            near_pass(*unit)
+
+        def subtract(unit):
+            t = staged("u_rows", [P, KP], BF16, 8)
+            nc.vector.tensor_tensor(
+                out=t[:].rearrange("p (u w e) -> p u w e", u=2, e=2),
+                in0=w_sb[unit].rearrange("p (w u e) -> p u w e", u=2, e=2),
+                in1=d_bank[unit][:].rearrange("p (w u e) -> p u w e", u=2, e=2),
+                op=ALU.subtract,
+            )
+            u_rows[unit] = t
+
+        def turn_updated(s):
+            for h in range(2):
+                b = bank("turn", [P, 2, 2, P])
+                for j in range(2):
+                    words = u_rows[quads[s][2 * h + j]][:].bitcast(F32)
+                    for u in range(2):
+                        nc.tensor.transpose(b[:, u, j, :], words[:, u * P : (u + 1) * P], ident[:])
+                u_bank[s, h] = b
+
+        def copy_updated(s):
+            t = staged("u_bf", [P, QUAD * P, 4], BF16, 2)
+            u_bf[s] = t
+            for h in range(2):
+                nc.scalar.copy(
+                    out=t[:, 2 * h * P : 2 * (h + 1) * P, :].bitcast(F32),
+                    in_=u_bank[s, h][:].rearrange("p u j r -> p (j r) u"),
+                )
+
+        def quantize_updated(s):
+            codes, scales = quantize("u%d" % s, u_bf[s][:].rearrange("p r t -> p (r t)"), QUAD * P)
+            for j in range(QUAD):
+                u_codes[quads[s][j]] = (codes[:, j * P : (j + 1) * P], scales[:, j * P : (j + 1) * P])
+
+        def apply_tokens(m):
+            y_bank[m] = bank("acc", [P, T])
+            for g in range(CHUNKS):
+                codes, scales = u_codes[m, g]
+                nc.tensor.matmul_mx(
+                    out=y_bank[m][:],
+                    lhsT=codes.bitcast(FP8X4),
+                    lhsT_scale=scales,
+                    rhs=x_sb[:, g, :].bitcast(FP4X4),
+                    rhs_scale=x_plane[:, g, :],
+                    start=(g == 0),
+                    stop=(g == CHUNKS - 1),
+                )
+
+        def store(m):
+            t = staged("y_sb", [P, T], F32, 3)
+            nc.scalar.copy(out=t[:], in_=y_bank[m][:])
+            nc.sync.dma_start(out=out[m * P : (m + 1) * P, :], in_=t[:])
+
+        q = quads[0]
+        turn_gone(0)
+        scale_errors(0)
+        quantize_errors(0, "near")
+        interleave_inv(0, VEC_COLS0)
+        quantize_errors(0, "far")
+        quantize_inv(0)
+        far_passes(*q[0])
+        turn_gone(1)
+        near_pass(*q[0])
+        scale_errors(1)
+        interleave_inv(1, 0)
+        subtract(q[0])
+        quantize_errors(1, "near")
+        quantize_errors(1, "far")
+        turn_gone(2)
+        update(q[1])
+        scale_errors(2)
+        subtract(q[1])
+        quantize_errors(2, "near")
+        quantize_errors(2, "far")
+        quantize_inv(1)
+        update(q[2])
+        interleave_inv(2, 0)
+        update(q[3])
+        subtract(q[2])
+        subtract(q[3])
+
+        for s in range(1, ROW_TILES):
+            q = quads[s]
+            nxt = s + 1 if HEAD <= s + 1 < ROW_TILES else None
+            update(q[0])
+            if nxt is not None:
+                turn_gone(nxt)
+            turn_updated(s - 1)
+            subtract(q[0])
+            if s < HEAD:
+                quantize_inv(s + 1)
+            if nxt is not None:
+                scale_errors(nxt)
+            copy_updated(s - 1)
+            if s == 1:
+                interleave_inv(3, 0)
+            if SORT_FROM <= s + 2 < ROW_TILES:
+                sort_gone(s + 2)
+            update(q[1])
+            subtract(q[1])
+            quantize_updated(s - 1)
+            if nxt is not None:
+                quantize_errors(nxt, "near")
+                quantize_errors(nxt, "far")
+            update(q[2])
+            update(q[3])
+            subtract(q[2])
+            subtract(q[3])
+            if s >= LAG:
+                apply_tokens(s - LAG)
+                store(s - LAG)
+
+        last = ROW_TILES - 1
+        turn_updated(last)
+        copy_updated(last)
+        quantize_updated(last)
+        for m in range(ROW_TILES - LAG, ROW_TILES):
+            apply_tokens(m)
+            store(m)

@@ -19,20 +19,25 @@ P = 128
 KP = 512
 ROW_TILES = M // P
 CHUNKS = C // KP
-HEAD = 3
+HEAD = 4
 QUAD = 4
-LAG = 3
-SORT_FROM = 4
-VEC_COLS0 = 288
+LAG = 4
+SORTED = (1, 2, 5, 6, 7)
+WARM = (0, 0, 0)
+VEC_COLS0 = 0
+RUN0 = 13
+D1 = 2
+LATE = (11, 13, 15, 17)
+V1 = 128
+QD = 3
 
 
 def tile_sparsegpt_lazy_update_s3_kernel(
     tc, w_rest, gone_near, rd_near, inv_near, gone_far, rd_far, far_words, far_scales, x_words, x_scales, out
 ):
     nc = tc.nc
-    units = [(m, c) for c in range(CHUNKS) for m in range(HEAD)]
-    units = units + [(m, c) for m in range(HEAD, ROW_TILES) for c in range(CHUNKS)]
-    quads = [units[i : i + QUAD] for i in range(0, len(units), QUAD)]
+    units = [(m, c) for c in range(CHUNKS) for m in range(ROW_TILES)]
+    quads = [units[i : i + QUAD] for i in (4, 8, 12, 0, 16, 20, 24, 28)]
 
     with ExitStack() as ctx:
         keep = ctx.enter_context(tc.tile_pool(name="keep", bufs=1))
@@ -74,8 +79,8 @@ def tile_sparsegpt_lazy_update_s3_kernel(
             rd[part] = kept("rd_" + part, [P, passes[part], 1, 4], BF16)
             nc.scalar.dma_start(out=rd[part][:, :, 0, :], in_=vec.rearrange("(g p t) -> p g t", p=P, t=4))
 
-        def load_gone(m):
-            for part in ("near", "far"):
+        def load_gone(m, parts=("far", "near")):
+            for part in parts:
                 gone[m, part] = kept("gone_%s%d" % (part, m), [P, passes[part] * KP], BF16)
                 nc.sync.dma_start(out=gone[m, part][:], in_=gone_hbm[part][m * P : (m + 1) * P, :])
 
@@ -99,50 +104,45 @@ def tile_sparsegpt_lazy_update_s3_kernel(
                     in_=rows[:, 4 * q : 4 * q + 4, :].rearrange("g r n -> r g n"),
                 )
 
-        def load_w_head(c):
-            t = kept("w_head%d" % c, [P, HEAD, KP], BF16)
-            nc.sync.dma_start(
-                out=t[:], in_=w_rest[0 : HEAD * P, c * KP : (c + 1) * KP].rearrange("(m p) n -> p m n", p=P)
-            )
-            for m in range(HEAD):
-                w_sb[m, c] = t[:, m, :]
-
-        def load_w(m):
-            t = kept("w_row%d" % m, [P, C], BF16)
-            nc.sync.dma_start(out=t[:], in_=w_rest[m * P : (m + 1) * P, :])
-            for c in range(CHUNKS):
-                w_sb[m, c] = t[:, c * KP : (c + 1) * KP]
+        def load_w(c, h):
+            t = kept("w_sb%d_%d" % (c, h), [P, 4, KP], BF16)
+            rows = w_rest[4 * h * P : 4 * (h + 1) * P, c * KP : (c + 1) * KP]
+            nc.sync.dma_start(out=t[:], in_=rows.rearrange("(m p) n -> p m n", p=P))
+            for j in range(4):
+                w_sb[4 * h + j, c] = t[:, j, :]
 
         far_rows = far_scales.bitcast(I32)
-        load_rd("near", rd_near)
-        load_rd("far", rd_far)
         load_gone(0)
-        load_inv(0)
+        load_rd("far", rd_far)
+        load_rd("near", rd_near)
+        load_gone(1)
         load_far(0)
         load_scale_rows(nc.scalar, far_plane[0], far_rows[:, :, 0:256])
-        load_gone(1)
-        load_inv(1)
-        load_w_head(0)
         load_gone(2)
+        load_inv(0)
+        load_gone(3)
+        load_gone(4)
+        load_gone(5)
+        load_inv(1)
+        load_gone(6)
+        load_gone(7)
         load_far(1)
+        load_w(0, 1)
+        load_w(1, 0)
+        load_w(0, 0)
         load_inv(2)
-        load_w_head(1)
+        load_w(1, 1)
         load_scale_rows(nc.sync, far_plane[1], far_rows[:, :, 256:512])
         load_far(2)
+        load_w(2, 0)
         load_inv(3)
-        load_w_head(2)
+        load_w(2, 1)
         load_far(3)
-        load_gone(3)
-        load_w_head(3)
-        load_w(3)
-        load_gone(4)
+        load_w(3, 0)
+        load_w(3, 1)
         load_scale_rows(nc.sync, x_plane, x_scales.bitcast(I32))
         x_sb = kept("x_sb", [P, CHUNKS, 2 * T], U8)
         nc.sync.dma_start(out=x_sb[:].bitcast(I32), in_=x_words.bitcast(I32).rearrange("g p n -> p g n"))
-        for m in range(4, ROW_TILES):
-            load_w(m)
-            if m + 1 < ROW_TILES:
-                load_gone(m + 1)
 
         sorted_words = {}
         e_bank = {}
@@ -163,30 +163,30 @@ def tile_sparsegpt_lazy_update_s3_kernel(
             nc.vector.quantize_mx(out=codes[:].bitcast(FP8X4), scales=scales[:], in_=src)
             return codes, scales
 
-        def sort_gone(m):
-            for part in ("near", "far"):
-                t = staged("sorted_" + part, [P, passes[part], 2, P], F32, 2)
+        def sort_gone(m, parts=("far", "near")):
+            for part in parts if m in SORTED else ():
+                t = staged("sorted_" + part, [P, passes[part], 2, P], F32, 3)
                 nc.scalar.copy(
                     out=t[:], in_=gone[m, part][:].bitcast(F32).rearrange("p (g w u) -> p g u w", w=P, u=2)
                 )
                 sorted_words[m, part] = t
 
-        def turn_gone(m):
-            for part in ("near", "far"):
+        def turn_gone(m, parts=("far", "near")):
+            for part in parts:
                 b = bank("turn", [P, 2, passes[part], P])
                 for g in range(passes[part]):
                     for u in range(2):
-                        if m >= SORT_FROM:
+                        if m in SORTED:
                             src = sorted_words[m, part][:, g, u, :]
                         else:
                             src = gone[m, part][:].bitcast(F32)[:, 256 * g + u : 256 * (g + 1) : 2]
                         nc.tensor.transpose(b[:, u, g, :], src, ident[:])
                 e_bank[m, part] = b
 
-        def scale_errors(m):
-            for part in ("near", "far"):
+        def scale_errors(m, parts=("far", "near")):
+            for part in parts:
                 n = passes[part]
-                t = staged("e_bf_" + part, [P, n, P, 4], BF16, 2)
+                t = staged("e_bf_" + part, [P, n, P, 4], BF16, 3)
                 nc.vector.tensor_tensor(
                     out=t[:].rearrange("p g r (u e) -> p (g r) u e", e=2),
                     in0=e_bank[m, part][:].bitcast(BF16).rearrange("p u g (r e) -> p (g r) u e", e=2),
@@ -243,12 +243,24 @@ def tile_sparsegpt_lazy_update_s3_kernel(
             far_passes(*unit)
             near_pass(*unit)
 
+        d_sorted = {}
+
+        def park(unit):
+            t = kept("parked%d" % unit[0], [P, KP], F32)
+            nc.scalar.copy(
+                out=t[:].rearrange("p (u w e) -> p u w e", u=2, e=2),
+                in_=d_bank[unit][:].rearrange("p (w u e) -> p u w e", u=2, e=2),
+            )
+            d_sorted[unit] = t[:].rearrange("p (u w e) -> p u w e", u=2, e=2)
+
         def subtract(unit):
-            t = staged("u_rows", [P, KP], BF16, 8)
+            if unit not in d_sorted:
+                d_sorted[unit] = d_bank[unit][:].rearrange("p (w u e) -> p u w e", u=2, e=2)
+            t = staged("u_rows", [P, KP], BF16, 16)
             nc.vector.tensor_tensor(
                 out=t[:].rearrange("p (u w e) -> p u w e", u=2, e=2),
                 in0=w_sb[unit].rearrange("p (w u e) -> p u w e", u=2, e=2),
-                in1=d_bank[unit][:].rearrange("p (w u e) -> p u w e", u=2, e=2),
+                in1=d_sorted[unit],
                 op=ALU.subtract,
             )
             u_rows[unit] = t
@@ -263,7 +275,7 @@ def tile_sparsegpt_lazy_update_s3_kernel(
                 u_bank[s, h] = b
 
         def copy_updated(s):
-            t = staged("u_bf", [P, QUAD * P, 4], BF16, 2)
+            t = staged("u_bf", [P, QUAD * P, 4], BF16, 3)
             u_bf[s] = t
             for h in range(2):
                 nc.scalar.copy(
@@ -295,69 +307,112 @@ def tile_sparsegpt_lazy_update_s3_kernel(
             nc.scalar.copy(out=t[:], in_=y_bank[m][:])
             nc.sync.dma_start(out=out[m * P : (m + 1) * P, :], in_=t[:])
 
-        q = quads[0]
+        def scale_and_quantize(m):
+            scale_errors(m)
+            scale_errors(m + 1, ["far"])
+            quantize_errors(m, "far")
+            quantize_errors(m, "near")
+            scale_errors(m + 1, ["near"])
+            quantize_errors(m + 1, "far")
+            quantize_errors(m + 1, "near")
+
+        def errors(m):
+            scale_errors(m)
+            quantize_errors(m, "far")
+            quantize_errors(m, "near")
+
+        sort_gone(1)
         turn_gone(0)
-        scale_errors(0)
-        quantize_errors(0, "near")
-        interleave_inv(0, VEC_COLS0)
-        quantize_errors(0, "far")
-        quantize_inv(0)
-        far_passes(*q[0])
+        errors(0)
         turn_gone(1)
-        near_pass(*q[0])
-        scale_errors(1)
-        interleave_inv(1, 0)
-        subtract(q[0])
-        quantize_errors(1, "near")
-        quantize_errors(1, "far")
+        errors(1)
+        far_passes(0, 0)
+        far_passes(1, 0)
+        sort_gone(2)
         turn_gone(2)
-        update(q[1])
-        scale_errors(2)
-        subtract(q[1])
-        quantize_errors(2, "near")
-        quantize_errors(2, "far")
-        quantize_inv(1)
-        update(q[2])
+        errors(2)
+        interleave_inv(0, VEC_COLS0)
+        turn_gone(3)
+        far_passes(2, 0)
+        errors(3)
+        quantize_inv(0)
+        turn_gone(4)
+        far_passes(3, 0)
+        near_pass(0, 0)
+        near_pass(1, 0)
+        near_pass(2, 0)
+        near_pass(3, 0)
+        sort_gone(5)
+        park((0, 0))
+        park((1, 0))
+        errors(4)
+        turn_gone(5)
+        errors(5)
+        update((4, 0))
+        sort_gone(6)
+        sort_gone(7)
+        turn_gone(6)
+        turn_gone(7)
+        park((2, 0))
+        park((3, 0))
+        interleave_inv(1, V1)
+        update((5, 0))
+        errors(6)
+        errors(7)
+        update(units[6])
+        update(units[7])
         interleave_inv(2, 0)
-        update(q[3])
-        subtract(q[2])
-        subtract(q[3])
-
-        for s in range(1, ROW_TILES):
-            q = quads[s]
-            nxt = s + 1 if HEAD <= s + 1 < ROW_TILES else None
-            update(q[0])
-            if nxt is not None:
-                turn_gone(nxt)
-            turn_updated(s - 1)
-            subtract(q[0])
-            if s < HEAD:
-                quantize_inv(s + 1)
-            if nxt is not None:
-                scale_errors(nxt)
-            copy_updated(s - 1)
-            if s == 1:
+        subtract(units[4])
+        quantize_inv(1)
+        subtract(units[5])
+        late = [0, 1, 2, 3]
+        runs = {RUN0: [0, 1], RUN0 + 8 - D1: [2, 3], 25: [4, 5], 29: [6]}
+        for i in range(8, 32):
+            update(units[i])
+            subtract(units[i - 2])
+            if late and i in LATE:
+                subtract(units[late[0]])
+                late = late[1:]
+            if i in (12, 20):
+                quantize_inv(i // 8 + 1)
+            if i == RUN0 + 1:
                 interleave_inv(3, 0)
-            if SORT_FROM <= s + 2 < ROW_TILES:
-                sort_gone(s + 2)
-            update(q[1])
-            subtract(q[1])
-            quantize_updated(s - 1)
-            if nxt is not None:
-                quantize_errors(nxt, "near")
-                quantize_errors(nxt, "far")
-            update(q[2])
-            update(q[3])
-            subtract(q[2])
-            subtract(q[3])
-            if s >= LAG:
-                apply_tokens(s - LAG)
-                store(s - LAG)
-
-        last = ROW_TILES - 1
-        turn_updated(last)
-        copy_updated(last)
-        quantize_updated(last)
-        for m in range(ROW_TILES - LAG, ROW_TILES):
+            for s in runs.get(i, []):
+                turn_updated(s)
+            for s in runs.get(i, []):
+                copy_updated(s)
+            for s in runs.get(i - QD, []):
+                quantize_updated(s)
+        subtract(units[30])
+        quantize_updated(6)
+        subtract(units[31])
+        apply_tokens(0)
+        turn_updated(7)
+        store(0)
+        copy_updated(7)
+        quantize_updated(7)
+        for m in range(1, ROW_TILES - 1):
             apply_tokens(m)
             store(m)
+        m = ROW_TILES - 1
+        for h in range(2):
+            half = bank("acc", [P, 2, P])
+            for j in range(2):
+                n = 2 * h + j
+                for g in range(CHUNKS):
+                    codes, scales = u_codes[m, g]
+                    nc.tensor.matmul_mx(
+                        out=half[:, j, :],
+                        lhsT=codes.bitcast(FP8X4),
+                        lhsT_scale=scales,
+                        rhs=x_sb[:, g, 2 * n * P : 2 * (n + 1) * P].bitcast(FP4X4),
+                        rhs_scale=x_plane[:, g, n * P : (n + 1) * P],
+                        start=(g == 0),
+                        stop=(g == CHUNKS - 1),
+                    )
+            y_half = kept("y_half%d" % h, [P, 2 * P], F32)
+            if h == 0:
+                nc.scalar.copy(out=y_half[:], in_=half[:].rearrange("p j n -> p (j n)"))
+            else:
+                nc.vector.tensor_copy(out=y_half[:], in_=half[:].rearrange("p j n -> p (j n)"))
+            nc.sync.dma_start(out=out[m * P : (m + 1) * P, 2 * h * P : 2 * (h + 1) * P], in_=y_half[:])

from contextlib import ExitStack

import concourse.mybir as mybir
from concourse.masks import make_identity

M, A, B, C, T = 1024, 512, 1024, 2048, 512
FLOPS = 2 * M * (A + B) * C + 2 * M * C * T

F32 = mybir.dt.float32
BF16 = mybir.dt.bfloat16
I32 = mybir.dt.int32
U32 = mybir.dt.uint32
U8 = mybir.dt.uint8
FP8X4 = mybir.dt.float8_e4m3fn_x4
FP4X4 = mybir.dt.float4_e2m1fn_x4
ALU = mybir.AluOpType

P = 128
KP = 512
ROW_TILES = M // P
CHUNKS = C // KP
HEAD = 4
QUAD = 4
LAG = 4
SORTED = (1, 2, 5, 6, 7)
WARM = (0, 0, 0)
VEC_COLS0 = 0
RUN0 = 13
D1 = 2
LATE = (11, 13, 15, 17)
V1 = 128
QD = 3


def tile_sparsegpt_lazy_update_s3_kernel(
    tc, w_rest, gone_near, rd_near, inv_near, gone_far, rd_far, far_words, far_scales, x_words, x_scales, out
):
    nc = tc.nc
    units = [(m, c) for c in range(CHUNKS) for m in range(ROW_TILES)]
    quads = [units[i : i + QUAD] for i in (4, 8, 12, 0, 16, 20, 24, 28)]

    with ExitStack() as ctx:
        keep = ctx.enter_context(tc.tile_pool(name="keep", bufs=1))
        stage = ctx.enter_context(tc.tile_pool(name="stage", bufs=2))
        psum = ctx.enter_context(tc.psum_pool(name="psum", bufs=1))
        ctx.enter_context(tc.manual_schedule())

        def kept(name, shape, dtype):
            return keep.tile(shape, dtype, name=name, align_bytes=64)

        def staged(tag, shape, dtype, bufs):
            return stage.tile(shape, dtype, name=tag, tag=tag, bufs=bufs, align_bytes=64)

        bank_uses = {"acc": 0, "turn": 0}

        def bank(kind, shape):
            tag = "%s%d" % (kind, bank_uses[kind] % 4)
            bank_uses[kind] = bank_uses[kind] + 1
            return psum.tile(shape, F32, name=tag, tag=tag)

        ident = kept("ident", [P, P], F32)
        make_identity(nc, ident[:])

        far_plane = [kept("far_plane%d" % h, [P, 2, 2 * KP], U8) for h in range(2)]
        x_plane = kept("x_plane", [P, CHUNKS, T], U8)
        for h in range(2):
            nc.vector.memset(far_plane[h][:].bitcast(I32), 0)
        nc.gpsimd.memset(x_plane[:].bitcast(I32), 0)

        gone = {}
        rd = {}
        w_sb = {}
        inv_raw = {}
        far_sb = {}
        passes = {"near": 1, "far": 2}
        gone_hbm = {"near": gone_near, "far": gone_far}

        def load_rd(part, vec):
            rd[part] = kept("rd_" + part, [P, passes[part], 1, 4], BF16)
            nc.scalar.dma_start(out=rd[part][:, :, 0, :], in_=vec.rearrange("(g p t) -> p g t", p=P, t=4))

        def load_gone(m, parts=("far", "near")):
            for part in parts:
                gone[m, part] = kept("gone_%s%d" % (part, m), [P, passes[part] * KP], BF16)
                nc.sync.dma_start(out=gone[m, part][:], in_=gone_hbm[part][m * P : (m + 1) * P, :])

        def load_inv(c):
            inv_raw[c] = kept("inv_raw%d" % c, [P, 4, KP], BF16)
            nc.sync.dma_start(
                out=inv_raw[c][:], in_=inv_near[:, c * KP : (c + 1) * KP].rearrange("(p t) n -> p t n", t=4)
            )

        def load_far(c):
            far_sb[c] = kept("far_sb%d" % c, [P, 2, 2 * KP], U8)
            nc.sync.dma_start(
                out=far_sb[c][:].bitcast(I32),
                in_=far_words.bitcast(I32)[:, :, c * 256 : (c + 1) * 256].rearrange("g p n -> p g n"),
            )

        def load_scale_rows(queue, plane, rows):
            for q in range(4):
                queue.dma_start(
                    out=plane[32 * q : 32 * q + 4, :, :].bitcast(I32),
                    in_=rows[:, 4 * q : 4 * q + 4, :].rearrange("g r n -> r g n"),
                )

        def load_w(c, h):
            t = kept("w_sb%d_%d" % (c, h), [P, 4, KP], BF16)
            rows = w_rest[4 * h * P : 4 * (h + 1) * P, c * KP : (c + 1) * KP]
            nc.sync.dma_start(out=t[:], in_=rows.rearrange("(m p) n -> p m n", p=P))
            for j in range(4):
                w_sb[4 * h + j, c] = t[:, j, :]

        far_rows = far_scales.bitcast(I32)
        load_gone(0)
        load_rd("far", rd_far)
        load_rd("near", rd_near)
        load_gone(1)
        load_far(0)
        load_scale_rows(nc.scalar, far_plane[0], far_rows[:, :, 0:256])
        load_gone(2)
        load_inv(0)
        load_gone(3)
        load_gone(4)
        load_gone(5)
        load_inv(1)
        load_gone(6)
        load_gone(7)
        load_far(1)
        load_w(0, 1)
        load_w(1, 0)
        load_w(0, 0)
        load_inv(2)
        load_w(1, 1)
        load_scale_rows(nc.sync, far_plane[1], far_rows[:, :, 256:512])
        load_far(2)
        load_w(2, 0)
        load_inv(3)
        load_w(2, 1)
        load_far(3)
        load_w(3, 0)
        load_w(3, 1)
        load_scale_rows(nc.sync, x_plane, x_scales.bitcast(I32))
        x_sb = kept("x_sb", [P, CHUNKS, 2 * T], U8)
        nc.sync.dma_start(out=x_sb[:].bitcast(I32), in_=x_words.bitcast(I32).rearrange("g p n -> p g n"))

        sorted_words = {}
        e_bank = {}
        e_bf = {}
        e_codes = {}
        inv_bf = {}
        inv_codes = {}
        d_bank = {}
        u_rows = {}
        u_bank = {}
        u_bf = {}
        u_codes = {}
        y_bank = {}

        def quantize(name, src, width):
            codes = kept(name + "_codes", [P, width], U32)
            scales = kept(name + "_scales", [P, width], U8)
            nc.vector.quantize_mx(out=codes[:].bitcast(FP8X4), scales=scales[:], in_=src)
            return codes, scales

        def sort_gone(m, parts=("far", "near")):
            for part in parts if m in SORTED else ():
                t = staged("sorted_" + part, [P, passes[part], 2, P], F32, 3)
                nc.scalar.copy(
                    out=t[:], in_=gone[m, part][:].bitcast(F32).rearrange("p (g w u) -> p g u w", w=P, u=2)
                )
                sorted_words[m, part] = t

        def turn_gone(m, parts=("far", "near")):
            for part in parts:
                b = bank("turn", [P, 2, passes[part], P])
                for g in range(passes[part]):
                    for u in range(2):
                        if m in SORTED:
                            src = sorted_words[m, part][:, g, u, :]
                        else:
                            src = gone[m, part][:].bitcast(F32)[:, 256 * g + u : 256 * (g + 1) : 2]
                        nc.tensor.transpose(b[:, u, g, :], src, ident[:])
                e_bank[m, part] = b

        def scale_errors(m, parts=("far", "near")):
            for part in parts:
                n = passes[part]
                t = staged("e_bf_" + part, [P, n, P, 4], BF16, 3)
                nc.vector.tensor_tensor(
                    out=t[:].rearrange("p g r (u e) -> p (g r) u e", e=2),
                    in0=e_bank[m, part][:].bitcast(BF16).rearrange("p u g (r e) -> p (g r) u e", e=2),
                    in1=rd[part][:].broadcast_to([P, n, P, 4]),
                    op=ALU.mult,
                )
                e_bf[m, part] = t

        def quantize_errors(m, part):
            src = e_bf[m, part][:].rearrange("p g r t -> p (g r t)")
            e_codes[m, part] = quantize("e_%s%d" % (part, m), src, passes[part] * P)

        def interleave_inv(c, vec_cols):
            t = staged("inv_bf", [P, KP, 4], BF16, 2)
            inv_bf[c] = t
            dst = t[:, vec_cols:KP, :].rearrange("p (n i) t -> p n t i", i=4)
            nc.scalar.copy(out=dst, in_=inv_raw[c][:, :, vec_cols:KP].rearrange("p t (n i) -> p n t i", i=4))
            if vec_cols > 0:
                dst = t[:, 0:vec_cols, :].rearrange("p (n i) t -> p n t i", i=4)
                nc.vector.tensor_copy(
                    out=dst, in_=inv_raw[c][:, :, 0:vec_cols].rearrange("p t (n i) -> p n t i", i=4)
                )

        def quantize_inv(c):
            inv_codes[c] = quantize("inv%d" % c, inv_bf[c][:].rearrange("p n t -> p (n t)"), KP)

        def far_passes(m, c):
            d_bank[m, c] = bank("acc", [P, KP])
            codes, scales = e_codes[m, "far"]
            for g in range(2):
                nc.tensor.matmul_mx(
                    out=d_bank[m, c][:],
                    lhsT=codes[:, g * P : (g + 1) * P].bitcast(FP8X4),
                    lhsT_scale=scales[:, g * P : (g + 1) * P],
                    rhs=far_sb[c][:, g, :].bitcast(FP4X4),
                    rhs_scale=far_plane[c // 2][:, g, (c % 2) * KP : (c % 2 + 1) * KP],
                    start=(g == 0),
                    stop=False,
                )

        def near_pass(m, c):
            codes, scales = e_codes[m, "near"]
            nc.tensor.matmul_mx(
                out=d_bank[m, c][:],
                lhsT=codes[:].bitcast(FP8X4),
                lhsT_scale=scales[:],
                rhs=inv_codes[c][0][:].bitcast(FP8X4),
                rhs_scale=inv_codes[c][1][:],
                start=False,
                stop=True,
            )

        def update(unit):
            far_passes(*unit)
            near_pass(*unit)

        d_sorted = {}

        def park(unit):
            t = kept("parked%d" % unit[0], [P, KP], F32)
            nc.scalar.copy(
                out=t[:].rearrange("p (u w e) -> p u w e", u=2, e=2),
                in_=d_bank[unit][:].rearrange("p (w u e) -> p u w e", u=2, e=2),
            )
            d_sorted[unit] = t[:].rearrange("p (u w e) -> p u w e", u=2, e=2)

        def subtract(unit):
            if unit not in d_sorted:
                d_sorted[unit] = d_bank[unit][:].rearrange("p (w u e) -> p u w e", u=2, e=2)
            t = staged("u_rows", [P, KP], BF16, 16)
            nc.vector.tensor_tensor(
                out=t[:].rearrange("p (u w e) -> p u w e", u=2, e=2),
                in0=w_sb[unit].rearrange("p (w u e) -> p u w e", u=2, e=2),
                in1=d_sorted[unit],
                op=ALU.subtract,
            )
            u_rows[unit] = t

        def turn_updated(s):
            for h in range(2):
                b = bank("turn", [P, 2, 2, P])
                for j in range(2):
                    words = u_rows[quads[s][2 * h + j]][:].bitcast(F32)
                    for u in range(2):
                        nc.tensor.transpose(b[:, u, j, :], words[:, u * P : (u + 1) * P], ident[:])
                u_bank[s, h] = b

        def copy_updated(s):
            t = staged("u_bf", [P, QUAD * P, 4], BF16, 3)
            u_bf[s] = t
            for h in range(2):
                nc.scalar.copy(
                    out=t[:, 2 * h * P : 2 * (h + 1) * P, :].bitcast(F32),
                    in_=u_bank[s, h][:].rearrange("p u j r -> p (j r) u"),
                )

        def quantize_updated(s):
            codes, scales = quantize("u%d" % s, u_bf[s][:].rearrange("p r t -> p (r t)"), QUAD * P)
            for j in range(QUAD):
                u_codes[quads[s][j]] = (codes[:, j * P : (j + 1) * P], scales[:, j * P : (j + 1) * P])

        def apply_tokens(m):
            y_bank[m] = bank("acc", [P, T])
            for g in range(CHUNKS):
                codes, scales = u_codes[m, g]
                nc.tensor.matmul_mx(
                    out=y_bank[m][:],
                    lhsT=codes.bitcast(FP8X4),
                    lhsT_scale=scales,
                    rhs=x_sb[:, g, :].bitcast(FP4X4),
                    rhs_scale=x_plane[:, g, :],
                    start=(g == 0),
                    stop=(g == CHUNKS - 1),
                )

        def store(m):
            t = staged("y_sb", [P, T], F32, 3)
            nc.scalar.copy(out=t[:], in_=y_bank[m][:])
            nc.sync.dma_start(out=out[m * P : (m + 1) * P, :], in_=t[:])

        def scale_and_quantize(m):
            scale_errors(m)
            scale_errors(m + 1, ["far"])
            quantize_errors(m, "far")
            quantize_errors(m, "near")
            scale_errors(m + 1, ["near"])
            quantize_errors(m + 1, "far")
            quantize_errors(m + 1, "near")

        def errors(m):
            scale_errors(m)
            quantize_errors(m, "far")
            quantize_errors(m, "near")

        sort_gone(1)
        turn_gone(0)
        errors(0)
        turn_gone(1)
        errors(1)
        far_passes(0, 0)
        far_passes(1, 0)
        sort_gone(2)
        turn_gone(2)
        errors(2)
        interleave_inv(0, VEC_COLS0)
        turn_gone(3)
        far_passes(2, 0)
        errors(3)
        quantize_inv(0)
        turn_gone(4)
        far_passes(3, 0)
        near_pass(0, 0)
        near_pass(1, 0)
        near_pass(2, 0)
        near_pass(3, 0)
        sort_gone(5)
        park((0, 0))
        park((1, 0))
        errors(4)
        turn_gone(5)
        errors(5)
        update((4, 0))
        sort_gone(6)
        sort_gone(7)
        turn_gone(6)
        turn_gone(7)
        park((2, 0))
        park((3, 0))
        interleave_inv(1, V1)
        update((5, 0))
        errors(6)
        errors(7)
        update(units[6])
        update(units[7])
        interleave_inv(2, 0)
        subtract(units[4])
        quantize_inv(1)
        subtract(units[5])
        late = [0, 1, 2, 3]
        runs = {RUN0: [0, 1], RUN0 + 8 - D1: [2, 3], 25: [4, 5], 29: [6]}
        for i in range(8, 32):
            update(units[i])
            subtract(units[i - 2])
            if late and i in LATE:
                subtract(units[late[0]])
                late = late[1:]
            if i in (12, 20):
                quantize_inv(i // 8 + 1)
            if i == RUN0 + 1:
                interleave_inv(3, 0)
            for s in runs.get(i, []):
                turn_updated(s)
            for s in runs.get(i, []):
                copy_updated(s)
            for s in runs.get(i - QD, []):
                quantize_updated(s)
        subtract(units[30])
        quantize_updated(6)
        subtract(units[31])
        apply_tokens(0)
        turn_updated(7)
        store(0)
        copy_updated(7)
        quantize_updated(7)
        for m in range(1, ROW_TILES - 1):
            apply_tokens(m)
            store(m)
        m = ROW_TILES - 1
        for h in range(2):
            half = bank("acc", [P, 2, P])
            for j in range(2):
                n = 2 * h + j
                for g in range(CHUNKS):
                    codes, scales = u_codes[m, g]
                    nc.tensor.matmul_mx(
                        out=half[:, j, :],
                        lhsT=codes.bitcast(FP8X4),
                        lhsT_scale=scales,
                        rhs=x_sb[:, g, 2 * n * P : 2 * (n + 1) * P].bitcast(FP4X4),
                        rhs_scale=x_plane[:, g, n * P : (n + 1) * P],
                        start=(g == 0),
                        stop=(g == CHUNKS - 1),
                    )
            y_half = kept("y_half%d" % h, [P, 2 * P], F32)
            if h == 0:
                nc.scalar.copy(out=y_half[:], in_=half[:].rearrange("p j n -> p (j n)"))
            else:
                nc.vector.tensor_copy(out=y_half[:], in_=half[:].rearrange("p j n -> p (j n)"))
            nc.sync.dma_start(out=out[m * P : (m + 1) * P, 2 * h * P : 2 * (h + 1) * P], in_=y_half[:])
